import numpy as np
import ml_dtypes


def mxq(x, axis, fmt="e4m3"):
    dtype, down = {"e4m3": (ml_dtypes.float8_e4m3fn, 7), "e5m2": (ml_dtypes.float8_e5m2, 14)}[fmt]
    v = np.moveaxis(np.asarray(x, np.float32).astype(ml_dtypes.bfloat16).astype(np.float64), axis, -1)
    blocks = v.reshape(v.shape[:-1] + (-1, 32))
    amax = np.abs(blocks).max(-1, keepdims=True)
    byte = np.maximum(np.where(amax > 0, np.frexp(amax)[1] - 1 + 127, 0) - down, 1)
    scale = np.exp2(byte - 127.0)
    codes = (blocks / scale).astype(np.float32).astype(dtype).astype(np.float64)
    return np.moveaxis((codes * scale).reshape(v.shape), -1, axis)


WIDE = False


def mx_kscale(k):
    if not WIDE:
        return np.ones(k)
    levels = np.array([10, -10, 5, -5, 0])
    if k % 512:
        return np.exp2(np.random.permutation(np.resize(levels, k // 32))).repeat(32)
    a = np.empty((k // 512, 16))
    for p in range(k // 512):
        a[p, :8] = np.random.permutation(np.resize(levels, 8))
        for g in range(8):
            far = levels[np.abs(levels - a[p, g]) >= 10]
            a[p, g + 8] = far[np.random.randint(len(far))]
    return np.exp2(a.ravel()).repeat(32)


def f64(x):
    return np.asarray(x).astype(np.float64)


def striped(idx):
    return np.tile(idx.reshape(-1, 16).T, (8, 1)).astype(np.uint16)


def unstriped(offs):
    return offs[:16].T.reshape(-1).astype(np.int64)


def striped8(idx):
    return np.concatenate([x.reshape(-1, 16).T for x in idx]).astype(np.uint16)


def runs(offs, k):
    lists = np.stack([offs[16 * r : 16 * r + 16].T.reshape(-1) for r in range(8)]).astype(np.int64)
    return lists[np.arange(k) % 512 // 64]


def pack_weight(w):
    k, n = w.shape
    w = f64(np.asarray(w, np.float32).astype(ml_dtypes.bfloat16)).reshape(k // 32, 32, n)
    amax = np.abs(w).max(1)
    byte = np.clip(np.where(amax > 0, np.frexp(amax)[1] - 1 + 127 - 7, 1), 1, 254)
    scaled = (w * np.exp2(127.0 - byte)[:, None, :]).reshape(k, n).astype(np.float32)
    words = np.ascontiguousarray(scaled.reshape(k // 512, 128, 4, n).transpose(0, 1, 3, 2)).astype(ml_dtypes.float8_e4m3fn).view(np.uint8)
    return words, np.ascontiguousarray(byte.astype(np.uint8).reshape(k // 512, 16, n))


def unpack_weight(words, scales):
    g, p, n, _ = words.shape
    vals = np.ascontiguousarray(words).view(ml_dtypes.float8_e4m3fn).astype(np.float64) * np.repeat(np.exp2(scales.astype(np.float64) - 127.0), 8, axis=1)[..., None]
    return vals.transpose(0, 1, 3, 2).reshape(g * 512, n)


E2M1 = np.array([0.0, 0.5, 1.0, 1.5, 2.0, 3.0, 4.0, 6.0, -0.0, -0.5, -1.0, -1.5, -2.0, -3.0, -4.0, -6.0])


def pack_fp4(w):
    k, n = w.shape
    w = f64(np.asarray(w, np.float32).astype(ml_dtypes.bfloat16)).reshape(k // 32, 32, n)
    amax = np.abs(w).max(1)
    mant, ex = np.frexp(amax / 6.0)
    byte = np.clip(np.where(amax > 0, np.where(mant > 0.5, ex, ex - 1) + 127, 1), 1, 254)
    scaled = (w * np.exp2(127.0 - byte)[:, None, :]).reshape(k, n).astype(np.float32)
    c = np.ascontiguousarray(scaled.reshape(k // 512, 128, 4, n).transpose(0, 1, 3, 2)).astype(ml_dtypes.float4_e2m1fn).view(np.uint8) & 0xF
    words = (c[..., 0::2] | (c[..., 1::2] << 4)).reshape(k // 512, 128, 2 * n)
    return np.ascontiguousarray(words), np.ascontiguousarray(byte.astype(np.uint8).reshape(k // 512, 16, n))


def unpack_fp4(words, scales):
    g, _, n = scales.shape
    words = np.ascontiguousarray(words).reshape(g, 128, n, 2)
    nib = np.empty((g, 128, n, 4), np.uint8)
    nib[..., 0::2] = words & 0xF
    nib[..., 1::2] = words >> 4
    vals = E2M1[nib] * np.repeat(np.exp2(scales.astype(np.float64) - 127.0), 8, axis=1)[..., None]
    return vals.transpose(0, 1, 3, 2).reshape(g * 512, n)


def sigmoid(v):
    return 1.0 / (1.0 + np.exp(-np.maximum(v, -700.0)))

def planes(y):
    n, m = y.shape
    v = y.astype(np.float32).astype(ml_dtypes.bfloat16).astype(np.float64).reshape(n // 32, 32, m)
    top = np.abs(v).max(1)
    byte = np.clip(np.where(top > 0, np.frexp(top)[1] - 1 + 127 - 7, 1), 1, 254)
    codes = (v * np.exp2(127.0 - byte)[:, None, :]).reshape(n, m).astype(np.float32).astype(ml_dtypes.float8_e4m3fn).view(np.uint8)
    words = codes.reshape(n // 512, 128, 4, m).transpose(0, 1, 3, 2)
    return np.ascontiguousarray(words), np.ascontiguousarray(byte.astype(np.uint8).reshape(n // 512, 16, m))


K, T, S, N, H, G = 512, 2048, 512, 512, 512, 2048


def setup_inputs():
    n = np.random.standard_normal
    s = mx_kscale(K)[:, None]
    u = mx_kscale(S)
    packed_xT = pack_weight(n((K, T)) * s)
    packed_w1 = pack_fp4(n((K, H)) / np.sqrt(K) / s)
    packed_w2 = pack_fp4(n((H, N)) / np.sqrt(H) / u[:, None])
    packed_dT = pack_weight(n((K, G)) / s)
    return {
        "x_words": packed_xT[0],
        "x_scales": packed_xT[1],
        "w1_words": packed_w1[0],
        "w1_scales": packed_w1[1],
        "gn": (np.random.uniform(0.5, 1.5, (H, 1)) * u[:, None]).astype(np.float32),
        "w2_words": packed_w2[0],
        "w2_scales": packed_w2[1],
        "d_words": packed_dT[0],
        "d_scales": packed_dT[1],
        "offs": striped(np.random.permutation(T)[:S]),
        "n1": striped8(np.stack([np.random.permutation(S) for _ in range(8)])),
        "n2": striped8(np.stack([np.random.permutation(S) for _ in range(8)])),
        "two": striped(np.random.permutation(T)[:S]),
        "k1": striped8(np.random.randint(0, G, (8, H))),
        "n3": striped(np.random.permutation(S)),
        "n4": striped(np.random.permutation(S)),
    }


def reference(x_words, x_scales, w1_words, w1_scales, gn, w2_words, w2_scales, d_words, d_scales, offs, n1, n2, two, k1, n3, n4):
    xq = unpack_weight(x_words, x_scales)[:, unstriped(offs)]
    y = unpack_fp4(w1_words, w1_scales).T @ xq
    z = f64(gn) * (np.maximum(y[np.arange(H)[:, None], runs(n1, H)], y[np.arange(H)[:, None], runs(n2, H)]) - (0.75 * y))
    a = unpack_fp4(w2_words, w2_scales).T @ mxq(z, 0, "e4m3")
    d_k1 = unpack_weight(d_words, d_scales)[np.arange(K)[:, None], runs(k1, K)]
    x_two = unpack_weight(x_words, x_scales)[:, unstriped(two)]
    b = 0.0625 * (d_k1.T @ x_two)
    out_0 = a * (sigmoid(b[:, unstriped(n4)])) - (0.5 * a[:, unstriped(n3)])
    return (out_0,) + planes(out_0)

@@ -1,0 +1,255 @@
+from contextlib import ExitStack
+
+import concourse.mybir as mybir
+
+FLOPS = 3 * 2 * 512 * 512 * 512
+
+F32 = mybir.dt.float32
+BF16 = mybir.dt.bfloat16
+I32 = mybir.dt.int32
+U32 = mybir.dt.uint32
+U16 = mybir.dt.uint16
+U8 = mybir.dt.uint8
+FP8X4 = mybir.dt.float8_e4m3fn_x4
+FP4X4 = mybir.dt.float4_e2m1fn_x4
+ALU = mybir.AluOpType
+ACT = mybir.ActivationFunctionType
+
+P = 128
+S = 512
+TABLE = 2048
+HALF = 256
+LIST_COLS = HALF // 16
+
+
+def tile_picked_cdjoingatebover_none_po_kernel(
+    tc, x_words, x_scales, w1_words, w1_scales, gn, w2_words, w2_scales, d_words, d_scales,
+    offs, n1, n2, two, k1, n3, n4, out_0, out_1, out_2,
+):
+    nc = tc.nc
+    with ExitStack() as ctx:
+        keep = ctx.enter_context(tc.tile_pool(name="keep", bufs=1))
+        psum = ctx.enter_context(tc.psum_pool(name="psum", bufs=1))
+
+        def sb(name, shape, dtype):
+            return keep.tile(shape, dtype, name=name, align_bytes=64)
+
+        def load_list(name, src):
+            t = sb(name, [P, S // 16], U16)
+            nc.sync.dma_start(t[:], src)
+            return t
+
+        def load_plane(queues, tile, src):
+            for q in range(4):
+                queues[q].dma_start(tile[32 * q : 32 * q + 4, :].bitcast(I32), src[0, 4 * q : 4 * q + 4, :].bitcast(I32))
+
+        def dealt_out(ap):
+            return ap.rearrange("p (t m) -> p t m", t=4)
+
+        def dealt_in(ap):
+            return ap.rearrange("p (m t) -> p t m", t=4)
+
+        def half_list(lst, h):
+            return lst[:, h * LIST_COLS : (h + 1) * LIST_COLS]
+
+        def gather(engine, out, window, entries):
+            src = window.indirect(entries)
+            if engine == "V":
+                nc.vector.tensor_copy(out, src)
+            else:
+                nc.scalar.activation(out, src, ACT.Copy)
+
+        xs = sb("xs", [P, TABLE], U8)
+        nc.gpsimd.memset(xs[:].bitcast(I32), 0)
+        w1s_raw = sb("w1s_raw", [P, S], U8)
+        nc.gpsimd.memset(w1s_raw[:].bitcast(I32), 0)
+        ds = sb("ds", [P, TABLE], U8)
+        nc.gpsimd.memset(ds[:].bitcast(I32), 0)
+        w2s_raw = sb("w2s_raw", [P, S], U8)
+        nc.gpsimd.memset(w2s_raw[:].bitcast(I32), 0)
+        dsp = sb("dsp", [P, S], U8)
+        nc.gpsimd.memset(dsp[:].bitcast(I32), 0)
+
+        l_offs = load_list("l_offs", offs)
+        xw = sb("xw", [P, TABLE], U32)
+        x_src = x_words[0].rearrange("p n t -> p (n t)").bitcast(I32)
+        nc.sync.dma_start(xw[:, : TABLE // 2].bitcast(I32), x_src[:, : TABLE // 2])
+        load_plane([nc.sync, nc.sync, nc.sync, nc.sync], xs, x_scales)
+        nc.sync.dma_start(xw[:, TABLE // 2 :].bitcast(I32), x_src[:, TABLE // 2 :])
+        w1w_raw = sb("w1w_raw", [P, 2 * S], U8)
+        nc.sync.dma_start(w1w_raw[:].bitcast(I32), w1_words[0].bitcast(I32))
+        load_plane([nc.sync, nc.sync, nc.sync, nc.sync], w1s_raw, w1_scales)
+        l_two = load_list("l_two", two)
+        l_n1 = load_list("l_n1", n1)
+        l_n2 = load_list("l_n2", n2)
+        dw = sb("dw", [P, TABLE], U32)
+        nc.sync.dma_start(dw[:].bitcast(I32), d_words[0].rearrange("p n t -> p (n t)").bitcast(I32))
+        l_k1 = load_list("l_k1", k1)
+        nc.sync.dma_start(ds[0:P:8, :].bitcast(I32), d_scales[0].bitcast(I32))
+        gain = sb("gain", [P, 4], F32)
+        nc.sync.dma_start(gain[:], gn.rearrange("(p t) o -> p (t o)", t=4))
+        w2w_raw = sb("w2w_raw", [P, 2 * S], U8)
+        nc.sync.dma_start(w2w_raw[:].bitcast(I32), w2_words[0].bitcast(I32))
+        load_plane([nc.sync, nc.sync, nc.sync, nc.sync], w2s_raw, w2_scales)
+        l_n4 = load_list("l_n4", n4)
+        l_n3 = load_list("l_n3", n3)
+
+        xq_s = sb("xq_s", [P, S], U8)
+        nc.vector.tensor_copy(xq_s[:], xs[:].indirect(l_offs[:]))
+        xq_w = sb("xq_w", [P, S], U32)
+        nc.vector.tensor_copy(xq_w[:], xw[:].indirect(l_offs[:]))
+        w1w = sb("w1w", [P, 2 * S], U8)
+        nc.scalar.copy(dealt_out(w1w[:].bitcast(U16)), dealt_in(w1w_raw[:].bitcast(U16)))
+        w1s = sb("w1s", [P, S], U8)
+        nc.vector.tensor_copy(dealt_out(w1s[:]), dealt_in(w1s_raw[:]))
+
+        y_ps = [psum.tile([P, S], F32, name=f"y_ps{t}", tag=f"bank{t}") for t in range(4)]
+        for t in range(4):
+            nc.tensor.matmul_mx(
+                y_ps[t][:], lhsT=w1w[:, 256 * t : 256 * (t + 1)].bitcast(FP4X4), lhsT_scale=w1s[:, P * t : P * (t + 1)],
+                rhs=xq_w[:].bitcast(FP8X4), rhs_scale=xq_s[:], start=True, stop=True)
+
+        xt_s = sb("xt_s", [P, S], U8)
+        nc.vector.tensor_copy(xt_s[:], xs[:].indirect(l_two[:]))
+        xt_w = sb("xt_w", [P, S], U32)
+        nc.vector.tensor_copy(xt_w[:], xw[:].indirect(l_two[:]))
+        dq_s = sb("dq_s", [P, S], U8)
+        nc.vector.tensor_copy(dq_s[:], ds[:].indirect(l_k1[:]))
+        dq_sd = sb("dq_sd", [P, S], U8)
+        nc.vector.tensor_copy(dealt_out(dq_sd[:]), dealt_in(dq_s[:]))
+        for a in range(4):
+            nc.sync.dma_start(dsp[a:P:32, :].bitcast(I32), dq_sd[8 * a : P : 32, :].bitcast(I32))
+        dq_w = sb("dq_w", [P, S], U32)
+        nc.vector.tensor_copy(dq_w[:], dw[:].indirect(l_k1[:]))
+        dq_wd = sb("dq_wd", [P, S], U32)
+        nc.vector.tensor_copy(dealt_out(dq_wd[:]), dealt_in(dq_w[:]))
+        b_ps = [psum.tile([P, S], F32, name=f"b_ps{t}", tag=f"bank{4 + t}") for t in range(4)]
+        for t in range(4):
+            nc.tensor.matmul_mx(
+                b_ps[t][:], lhsT=dq_wd[:, P * t : P * (t + 1)].bitcast(FP8X4), lhsT_scale=dsp[:, P * t : P * (t + 1)],
+                rhs=xt_w[:].bitcast(FP8X4), rhs_scale=xt_s[:], start=True, stop=True)
+        w2w = sb("w2w", [P, 2 * S], U8)
+        nc.scalar.copy(dealt_out(w2w[:].bitcast(U16)), dealt_in(w2w_raw[:].bitcast(U16)))
+        w2s = sb("w2s", [P, S], U8)
+        nc.vector.tensor_copy(dealt_out(w2s[:]), dealt_in(w2s_raw[:]))
+
+        y_sb = [sb(f"y_sb{t}", [P, S], F32) for t in range(4)]
+        g1 = sb("g1", [P, 4, S], F32)
+        g2 = sb("g2", [P, 4, S], F32)
+        top = sb("top", [P, 4, S], F32)
+        dif = sb("dif", [P, 4, S], F32)
+        z_bf = sb("z_bf", [P, S, 4], BF16)
+        z_w = sb("z_w", [P, S], U32)
+        z_s = sb("z_s", [P, S], U8)
+        planes = sb("planes", [P, 7 * S], F32)
+        a_last = sb("a_last", [P, S], F32)
+        sg = sb("sg", [P, 4, S], F32)
+        prod = sb("prod", [P, 4, S], F32)
+        g3 = sb("g3", [P, 3, S], F32)
+        res = sb("res", [P, 4, S], F32)
+        o_bf = [sb(f"o_bf{h}", [P, HALF, 4], BF16) for h in range(2)]
+        o_w = sb("o_w", [P, S], U32)
+        o_s = sb("o_s", [P, S], U8)
+        out_rows = out_0.rearrange("(p t) j -> p t j", t=4)
+        words_out = out_1[0].rearrange("p n t -> p (n t)").bitcast(I32)
+
+        def cols(h):
+            return slice(h * HALF, (h + 1) * HALF)
+
+        def plane(i, n=1):
+            return planes[:, i * S : (i + n) * S]
+
+        def a_plane(t):
+            return a_last[:] if t == 3 else plane(2 - t)
+
+        def y_gathers(e, t):
+            for h in range(2):
+                gather(e, g1[:, t, cols(h)], y_sb[t][:], half_list(l_n1, h))
+                gather(e, g2[:, t, cols(h)], y_sb[t][:], half_list(l_n2, h))
+
+        def z_top(ts):
+            nc.vector.tensor_tensor(top[:, ts, :], g1[:, ts, :], g2[:, ts, :], ALU.max)
+
+        def z_dif(t):
+            nc.vector.scalar_tensor_tensor(dif[:, t, :], y_sb[t][:], -0.75, top[:, t, :], ALU.mult, ALU.add)
+
+        def gate_half(e, h):
+            gather(e, sg[:, 0, cols(h)], plane(6), half_list(l_n4, h))
+
+        def gate_gather(e, t):
+            gather(e, sg[:, t, :], plane(6 - t, 2), l_n4[:])
+
+        def gate_product(t):
+            nc.vector.scalar_tensor_tensor(prod[:, t, :], sg[:, t, :], 1.0, a_plane(t), ALU.subtract, ALU.mult)
+
+        def join(t, cs):
+            nc.vector.tensor_tensor(res[:, t, cs], g3[:, t, cs], prod[:, t, cs], ALU.add)
+
+        def store(t):
+            nc.sync.dma_start(out_rows[:, t, :], res[:, t, :])
+
+        def fused_join(h):
+            nc.vector.tensor_tensor(res[:, 3, cols(h)], a_last[:].indirect(half_list(l_n3, h)), prod[:, 3, cols(h)], ALU.add)
+
+        def o_round(h):
+            copy = nc.scalar.copy if h == 0 else nc.vector.tensor_copy
+            copy(
+                o_bf[h][:].rearrange("p (c i) t -> p c t i", i=4),
+                res[:, :, cols(h)].rearrange("p t (c i) -> p c t i", i=4))
+
+        def o_quant(h):
+            nc.vector.quantize_mx(o_w[:, cols(h)].bitcast(FP8X4), o_s[:, cols(h)], o_bf[h][:].rearrange("p j t -> p (j t)"))
+            nc.sync.dma_start(words_out[:, cols(h)], o_w[:, cols(h)].bitcast(I32))
+
+        for t in range(3):
+            nc.scalar.copy(y_sb[t][:], y_ps[t][:])
+            y_gathers("S", t)
+            if t == 0:
+                nc.scalar.copy(y_sb[3][:], y_ps[3][:])
+        y_gathers("V", 3)
+        z_top(slice(0, 2))
+        z_dif(0)
+        z_dif(1)
+        z_top(slice(2, 4))
+        z_dif(3)
+        z_dif(2)
+        for t in range(4):
+            nc.scalar.activation(plane(6 - t), b_ps[t][:], ACT.Tanh, scale=-0.03125)
+        gate_half("S", 0)
+        for t in range(1, 4):
+            gate_gather("S", t)
+        nc.vector.tensor_tensor(
+            z_bf[:].rearrange("p (c i) t -> p c t i", i=4),
+            dif[:].rearrange("p t (c i) -> p c t i", i=4),
+            gain[:].unsqueeze(1).unsqueeze(3).to_broadcast([P, S // 4, 4, 4]),
+            ALU.mult)
+        nc.vector.quantize_mx(z_w[:].bitcast(FP8X4), z_s[:], z_bf[:].rearrange("p j t -> p (j t)"))
+        gate_half("V", 1)
+        for t in range(4):
+            a_ps = psum.tile([P, S], F32, name=f"a_ps{t}", tag=f"bank{t}")
+            nc.tensor.matmul_mx(
+                a_ps[:], lhsT=w2w[:, 256 * t : 256 * (t + 1)].bitcast(FP4X4), lhsT_scale=w2s[:, P * t : P * (t + 1)],
+                rhs=z_w[:].bitcast(FP8X4), rhs_scale=z_s[:], start=True, stop=True)
+            nc.scalar.activation(a_plane(t), a_ps[:], ACT.Copy, scale=-0.5)
+            gate_product(t)
+        for t in range(2):
+            gather("S", g3[:, t, :], plane(2 - t, 2), l_n3[:])
+        for h in range(2):
+            gather("S", g3[:, 2, cols(h)], plane(0), half_list(l_n3, h))
+        fused_join(0)
+        join(0, slice(0, S))
+        store(0)
+        fused_join(1)
+        store(3)
+        join(1, slice(0, S))
+        store(1)
+        join(2, cols(0))
+        o_round(0)
+        join(2, cols(1))
+        store(2)
+        o_round(1)
+        o_quant(0)
+        o_quant(1)
+        for q in range(4):
+            queue = nc.sync if q % 2 == 0 else nc.scalar
+            queue.dma_start(out_2[0, 4 * q : 4 * q + 4, :].bitcast(I32), o_s[32 * q : 32 * q + 4, :].bitcast(I32))

@@ -80,12 +80,12 @@ def tile_picked_cdjoingatebover_none_po_kernel(
         nc.sync.dma_start(w1w_raw[:].bitcast(I32), w1_words[0].bitcast(I32))
         load_plane([nc.sync, nc.sync, nc.sync, nc.sync], w1s_raw, w1_scales)
         l_two = load_list("l_two", two)
+        l_k1 = load_list("l_k1", k1)
+        nc.sync.dma_start(ds[0:P:8, :].bitcast(I32), d_scales[0].bitcast(I32))
         l_n1 = load_list("l_n1", n1)
         l_n2 = load_list("l_n2", n2)
         dw = sb("dw", [P, TABLE], U32)
         nc.sync.dma_start(dw[:].bitcast(I32), d_words[0].rearrange("p n t -> p (n t)").bitcast(I32))
-        l_k1 = load_list("l_k1", k1)
-        nc.sync.dma_start(ds[0:P:8, :].bitcast(I32), d_scales[0].bitcast(I32))
         gain = sb("gain", [P, 4], F32)
         nc.sync.dma_start(gain[:], gn.rearrange("(p t) o -> p (t o)", t=4))
         w2w_raw = sb("w2w_raw", [P, 2 * S], U8)
@@ -111,27 +111,28 @@ def tile_picked_cdjoingatebover_none_po_kernel(
 
         xt_s = sb("xt_s", [P, S], U8)
         nc.vector.tensor_copy(xt_s[:], xs[:].indirect(l_two[:]))
-        xt_w = sb("xt_w", [P, S], U32)
-        nc.vector.tensor_copy(xt_w[:], xw[:].indirect(l_two[:]))
         dq_s = sb("dq_s", [P, S], U8)
         nc.vector.tensor_copy(dq_s[:], ds[:].indirect(l_k1[:]))
+        xt_w = sb("xt_w", [P, S], U32)
+        nc.vector.tensor_copy(xt_w[:], xw[:].indirect(l_two[:]))
         dq_sd = sb("dq_sd", [P, S], U8)
         nc.vector.tensor_copy(dealt_out(dq_sd[:]), dealt_in(dq_s[:]))
         for a in range(4):
             nc.sync.dma_start(dsp[a:P:32, :].bitcast(I32), dq_sd[8 * a : P : 32, :].bitcast(I32))
         dq_w = sb("dq_w", [P, S], U32)
         nc.vector.tensor_copy(dq_w[:], dw[:].indirect(l_k1[:]))
+        w2w = sb("w2w", [P, 2 * S], U8)
+        nc.scalar.copy(dealt_out(w2w[:].bitcast(U16)), dealt_in(w2w_raw[:].bitcast(U16)))
+        w2s = sb("w2s", [P, S], U8)
+        nc.vector.tensor_copy(dealt_out(w2s[:]), dealt_in(w2s_raw[:]))
         dq_wd = sb("dq_wd", [P, S], U32)
-        nc.vector.tensor_copy(dealt_out(dq_wd[:]), dealt_in(dq_w[:]))
+        nc.vector.tensor_copy(
+            dq_wd[:].rearrange("p (t c i) -> p c t i", t=4, i=4), dq_w[:].rearrange("p (c i t) -> p c t i", t=4, i=4))
         b_ps = [psum.tile([P, S], F32, name=f"b_ps{t}", tag=f"bank{4 + t}") for t in range(4)]
         for t in range(4):
             nc.tensor.matmul_mx(
                 b_ps[t][:], lhsT=dq_wd[:, P * t : P * (t + 1)].bitcast(FP8X4), lhsT_scale=dsp[:, P * t : P * (t + 1)],
                 rhs=xt_w[:].bitcast(FP8X4), rhs_scale=xt_s[:], start=True, stop=True)
-        w2w = sb("w2w", [P, 2 * S], U8)
-        nc.scalar.copy(dealt_out(w2w[:].bitcast(U16)), dealt_in(w2w_raw[:].bitcast(U16)))
-        w2s = sb("w2s", [P, S], U8)
-        nc.vector.tensor_copy(dealt_out(w2s[:]), dealt_in(w2s_raw[:]))
 
         y_sb = [sb(f"y_sb{t}", [P, S], F32) for t in range(4)]
         g1 = sb("g1", [P, 4, S], F32)
@@ -162,16 +163,25 @@ def tile_picked_cdjoingatebover_none_po_kernel(
         def a_plane(t):
             return a_last[:] if t == 3 else plane(2 - t)
 
-        def y_gathers(e, t):
-            for h in range(2):
-                gather(e, g1[:, t, cols(h)], y_sb[t][:], half_list(l_n1, h))
-                gather(e, g2[:, t, cols(h)], y_sb[t][:], half_list(l_n2, h))
+        def y_gathers(e, t, h):
+            gather(e, g1[:, t, cols(h)], y_sb[t][:], half_list(l_n1, h))
+            gather(e, g2[:, t, cols(h)], y_sb[t][:], half_list(l_n2, h))
 
-        def z_top(ts):
-            nc.vector.tensor_tensor(top[:, ts, :], g1[:, ts, :], g2[:, ts, :], ALU.max)
+        def z_top(t, cs):
+            nc.vector.tensor_tensor(top[:, t, cs], g1[:, t, cs], g2[:, t, cs], ALU.max)
 
-        def z_dif(t):
-            nc.vector.scalar_tensor_tensor(dif[:, t, :], y_sb[t][:], -0.75, top[:, t, :], ALU.mult, ALU.add)
+        def z_dif(t, cs):
+            nc.vector.scalar_tensor_tensor(dif[:, t, cs], y_sb[t][:, cs], -0.75, top[:, t, cs], ALU.mult, ALU.add)
+
+        def z_round(h):
+            nc.vector.tensor_tensor(
+                z_bf[:, cols(h), :].rearrange("p (c i) t -> p c t i", i=4),
+                dif[:, :, cols(h)].rearrange("p t (c i) -> p c t i", i=4),
+                gain[:].unsqueeze(1).unsqueeze(3).to_broadcast([P, HALF // 4, 4, 4]),
+                ALU.mult)
+
+        def z_quant(h):
+            nc.vector.quantize_mx(z_w[:, cols(h)].bitcast(FP8X4), z_s[:, cols(h)], z_bf[:, cols(h), :].rearrange("p j t -> p (j t)"))
 
         def gate_half(e, h):
             gather(e, sg[:, 0, cols(h)], plane(6), half_list(l_n4, h))
@@ -201,47 +211,63 @@ def tile_picked_cdjoingatebover_none_po_kernel(
             nc.vector.quantize_mx(o_w[:, cols(h)].bitcast(FP8X4), o_s[:, cols(h)], o_bf[h][:].rearrange("p j t -> p (j t)"))
             nc.sync.dma_start(words_out[:, cols(h)], o_w[:, cols(h)].bitcast(I32))
 
-        for t in range(3):
+        def y_out(t):
             nc.scalar.copy(y_sb[t][:], y_ps[t][:])
-            y_gathers("S", t)
-            if t == 0:
-                nc.scalar.copy(y_sb[3][:], y_ps[3][:])
-        y_gathers("V", 3)
-        z_top(slice(0, 2))
-        z_dif(0)
-        z_dif(1)
-        z_top(slice(2, 4))
-        z_dif(3)
-        z_dif(2)
+
+        whole = slice(0, S)
+        y_out(0)
+        y_out(1)
+        y_gathers("S", 0, 0)
+        y_gathers("S", 0, 1)
+        y_out(3)
+        y_gathers("S", 1, 0)
+        y_out(2)
+        y_gathers("S", 1, 1)
+        y_gathers("S", 2, 0)
+        y_gathers("S", 2, 1)
+        z_top(0, whole)
+        y_gathers("V", 3, 0)
+        z_dif(0, whole)
+        y_gathers("V", 3, 1)
+        z_top(1, whole)
+        z_top(3, whole)
+        z_dif(1, whole)
+        z_top(2, cols(0))
+        z_dif(3, whole)
+        z_dif(2, cols(0))
+        z_top(2, cols(1))
+        z_round(0)
+        z_dif(2, cols(1))
+        z_quant(0)
+        z_round(1)
         for t in range(4):
             nc.scalar.activation(plane(6 - t), b_ps[t][:], ACT.Tanh, scale=-0.03125)
-        gate_half("S", 0)
-        for t in range(1, 4):
-            gate_gather("S", t)
-        nc.vector.tensor_tensor(
-            z_bf[:].rearrange("p (c i) t -> p c t i", i=4),
-            dif[:].rearrange("p t (c i) -> p c t i", i=4),
-            gain[:].unsqueeze(1).unsqueeze(3).to_broadcast([P, S // 4, 4, 4]),
-            ALU.mult)
-        nc.vector.quantize_mx(z_w[:].bitcast(FP8X4), z_s[:], z_bf[:].rearrange("p j t -> p (j t)"))
         gate_half("V", 1)
-        for t in range(4):
-            a_ps = psum.tile([P, S], F32, name=f"a_ps{t}", tag=f"bank{t}")
+        z_quant(1)
+        gate_gather("V", 3)
+        gate_half("S", 0)
+        for t in (1, 2):
+            gate_gather("S", t)
+        for t in (3, 0, 1, 2):
+            a_ps = psum.tile([P, S], F32, name=f"a_ps{t}", tag=f"bank{4 + t}")
             nc.tensor.matmul_mx(
                 a_ps[:], lhsT=w2w[:, 256 * t : 256 * (t + 1)].bitcast(FP4X4), lhsT_scale=w2s[:, P * t : P * (t + 1)],
                 rhs=z_w[:].bitcast(FP8X4), rhs_scale=z_s[:], start=True, stop=True)
             nc.scalar.activation(a_plane(t), a_ps[:], ACT.Copy, scale=-0.5)
-            gate_product(t)
         for t in range(2):
             gather("S", g3[:, t, :], plane(2 - t, 2), l_n3[:])
         for h in range(2):
             gather("S", g3[:, 2, cols(h)], plane(0), half_list(l_n3, h))
+        gate_product(3)
+        gate_product(0)
         fused_join(0)
-        join(0, slice(0, S))
-        store(0)
+        gate_product(1)
         fused_join(1)
         store(3)
-        join(1, slice(0, S))
+        gate_product(2)
+        join(0, whole)
+        store(0)
+        join(1, whole)
         store(1)
         join(2, cols(0))
         o_round(0)

from contextlib import ExitStack

import concourse.mybir as mybir

FLOPS = 3 * 2 * 512 * 512 * 512

F32 = mybir.dt.float32
BF16 = mybir.dt.bfloat16
I32 = mybir.dt.int32
U32 = mybir.dt.uint32
U16 = mybir.dt.uint16
U8 = mybir.dt.uint8
FP8X4 = mybir.dt.float8_e4m3fn_x4
FP4X4 = mybir.dt.float4_e2m1fn_x4
ALU = mybir.AluOpType
ACT = mybir.ActivationFunctionType

P = 128
S = 512
TABLE = 2048
HALF = 256
LIST_COLS = HALF // 16


def tile_picked_cdjoingatebover_none_po_kernel(
    tc, x_words, x_scales, w1_words, w1_scales, gn, w2_words, w2_scales, d_words, d_scales,
    offs, n1, n2, two, k1, n3, n4, out_0, out_1, out_2,
):
    nc = tc.nc
    with ExitStack() as ctx:
        keep = ctx.enter_context(tc.tile_pool(name="keep", bufs=1))
        psum = ctx.enter_context(tc.psum_pool(name="psum", bufs=1))

        def sb(name, shape, dtype):
            return keep.tile(shape, dtype, name=name, align_bytes=64)

        def load_list(name, src):
            t = sb(name, [P, S // 16], U16)
            nc.sync.dma_start(t[:], src)
            return t

        def load_plane(queues, tile, src):
            for q in range(4):
                queues[q].dma_start(tile[32 * q : 32 * q + 4, :].bitcast(I32), src[0, 4 * q : 4 * q + 4, :].bitcast(I32))

        def dealt_out(ap):
            return ap.rearrange("p (t m) -> p t m", t=4)

        def dealt_in(ap):
            return ap.rearrange("p (m t) -> p t m", t=4)

        def half_list(lst, h):
            return lst[:, h * LIST_COLS : (h + 1) * LIST_COLS]

        def gather(engine, out, window, entries):
            src = window.indirect(entries)
            if engine == "V":
                nc.vector.tensor_copy(out, src)
            else:
                nc.scalar.activation(out, src, ACT.Copy)

        xs = sb("xs", [P, TABLE], U8)
        nc.gpsimd.memset(xs[:].bitcast(I32), 0)
        w1s_raw = sb("w1s_raw", [P, S], U8)
        nc.gpsimd.memset(w1s_raw[:].bitcast(I32), 0)
        ds = sb("ds", [P, TABLE], U8)
        nc.gpsimd.memset(ds[:].bitcast(I32), 0)
        w2s_raw = sb("w2s_raw", [P, S], U8)
        nc.gpsimd.memset(w2s_raw[:].bitcast(I32), 0)
        dsp = sb("dsp", [P, S], U8)
        nc.gpsimd.memset(dsp[:].bitcast(I32), 0)

        l_offs = load_list("l_offs", offs)
        xw = sb("xw", [P, TABLE], U32)
        x_src = x_words[0].rearrange("p n t -> p (n t)").bitcast(I32)
        nc.sync.dma_start(xw[:, : TABLE // 2].bitcast(I32), x_src[:, : TABLE // 2])
        load_plane([nc.sync, nc.sync, nc.sync, nc.sync], xs, x_scales)
        nc.sync.dma_start(xw[:, TABLE // 2 :].bitcast(I32), x_src[:, TABLE // 2 :])
        w1w_raw = sb("w1w_raw", [P, 2 * S], U8)
        nc.sync.dma_start(w1w_raw[:].bitcast(I32), w1_words[0].bitcast(I32))
        load_plane([nc.sync, nc.sync, nc.sync, nc.sync], w1s_raw, w1_scales)
        l_two = load_list("l_two", two)
        l_k1 = load_list("l_k1", k1)
        nc.sync.dma_start(ds[0:P:8, :].bitcast(I32), d_scales[0].bitcast(I32))
        l_n1 = load_list("l_n1", n1)
        l_n2 = load_list("l_n2", n2)
        dw = sb("dw", [P, TABLE], U32)
        nc.sync.dma_start(dw[:].bitcast(I32), d_words[0].rearrange("p n t -> p (n t)").bitcast(I32))
        gain = sb("gain", [P, 4], F32)
        nc.sync.dma_start(gain[:], gn.rearrange("(p t) o -> p (t o)", t=4))
        w2w_raw = sb("w2w_raw", [P, 2 * S], U8)
        nc.sync.dma_start(w2w_raw[:].bitcast(I32), w2_words[0].bitcast(I32))
        load_plane([nc.sync, nc.sync, nc.sync, nc.sync], w2s_raw, w2_scales)
        l_n4 = load_list("l_n4", n4)
        l_n3 = load_list("l_n3", n3)

        xq_s = sb("xq_s", [P, S], U8)
        nc.vector.tensor_copy(xq_s[:], xs[:].indirect(l_offs[:]))
        xq_w = sb("xq_w", [P, S], U32)
        nc.vector.tensor_copy(xq_w[:], xw[:].indirect(l_offs[:]))
        w1w = sb("w1w", [P, 2 * S], U8)
        nc.scalar.copy(dealt_out(w1w[:].bitcast(U16)), dealt_in(w1w_raw[:].bitcast(U16)))
        w1s = sb("w1s", [P, S], U8)
        nc.vector.tensor_copy(dealt_out(w1s[:]), dealt_in(w1s_raw[:]))

        y_ps = [psum.tile([P, S], F32, name=f"y_ps{t}", tag=f"bank{t}") for t in range(4)]
        for t in range(4):
            nc.tensor.matmul_mx(
                y_ps[t][:], lhsT=w1w[:, 256 * t : 256 * (t + 1)].bitcast(FP4X4), lhsT_scale=w1s[:, P * t : P * (t + 1)],
                rhs=xq_w[:].bitcast(FP8X4), rhs_scale=xq_s[:], start=True, stop=True)

        xt_s = sb("xt_s", [P, S], U8)
        nc.vector.tensor_copy(xt_s[:], xs[:].indirect(l_two[:]))
        dq_s = sb("dq_s", [P, S], U8)
        nc.vector.tensor_copy(dq_s[:], ds[:].indirect(l_k1[:]))
        xt_w = sb("xt_w", [P, S], U32)
        nc.vector.tensor_copy(xt_w[:], xw[:].indirect(l_two[:]))
        dq_sd = sb("dq_sd", [P, S], U8)
        nc.vector.tensor_copy(dealt_out(dq_sd[:]), dealt_in(dq_s[:]))
        for a in range(4):
            nc.sync.dma_start(dsp[a:P:32, :].bitcast(I32), dq_sd[8 * a : P : 32, :].bitcast(I32))
        dq_w = sb("dq_w", [P, S], U32)
        nc.vector.tensor_copy(dq_w[:], dw[:].indirect(l_k1[:]))
        w2w = sb("w2w", [P, 2 * S], U8)
        nc.scalar.copy(dealt_out(w2w[:].bitcast(U16)), dealt_in(w2w_raw[:].bitcast(U16)))
        w2s = sb("w2s", [P, S], U8)
        nc.vector.tensor_copy(dealt_out(w2s[:]), dealt_in(w2s_raw[:]))
        dq_wd = sb("dq_wd", [P, S], U32)
        nc.vector.tensor_copy(
            dq_wd[:].rearrange("p (t c i) -> p c t i", t=4, i=4), dq_w[:].rearrange("p (c i t) -> p c t i", t=4, i=4))
        b_ps = [psum.tile([P, S], F32, name=f"b_ps{t}", tag=f"bank{4 + t}") for t in range(4)]
        for t in range(4):
            nc.tensor.matmul_mx(
                b_ps[t][:], lhsT=dq_wd[:, P * t : P * (t + 1)].bitcast(FP8X4), lhsT_scale=dsp[:, P * t : P * (t + 1)],
                rhs=xt_w[:].bitcast(FP8X4), rhs_scale=xt_s[:], start=True, stop=True)

        y_sb = [sb(f"y_sb{t}", [P, S], F32) for t in range(4)]
        g1 = sb("g1", [P, 4, S], F32)
        g2 = sb("g2", [P, 4, S], F32)
        top = sb("top", [P, 4, S], F32)
        dif = sb("dif", [P, 4, S], F32)
        z_bf = sb("z_bf", [P, S, 4], BF16)
        z_w = sb("z_w", [P, S], U32)
        z_s = sb("z_s", [P, S], U8)
        planes = sb("planes", [P, 7 * S], F32)
        a_last = sb("a_last", [P, S], F32)
        sg = sb("sg", [P, 4, S], F32)
        prod = sb("prod", [P, 4, S], F32)
        g3 = sb("g3", [P, 3, S], F32)
        res = sb("res", [P, 4, S], F32)
        o_bf = [sb(f"o_bf{h}", [P, HALF, 4], BF16) for h in range(2)]
        o_w = sb("o_w", [P, S], U32)
        o_s = sb("o_s", [P, S], U8)
        out_rows = out_0.rearrange("(p t) j -> p t j", t=4)
        words_out = out_1[0].rearrange("p n t -> p (n t)").bitcast(I32)

        def cols(h):
            return slice(h * HALF, (h + 1) * HALF)

        def plane(i, n=1):
            return planes[:, i * S : (i + n) * S]

        def a_plane(t):
            return a_last[:] if t == 3 else plane(2 - t)

        def y_gathers(e, t, h):
            gather(e, g1[:, t, cols(h)], y_sb[t][:], half_list(l_n1, h))
            gather(e, g2[:, t, cols(h)], y_sb[t][:], half_list(l_n2, h))

        def z_top(t, cs):
            nc.vector.tensor_tensor(top[:, t, cs], g1[:, t, cs], g2[:, t, cs], ALU.max)

        def z_dif(t, cs):
            nc.vector.scalar_tensor_tensor(dif[:, t, cs], y_sb[t][:, cs], -0.75, top[:, t, cs], ALU.mult, ALU.add)

        def z_round(h):
            nc.vector.tensor_tensor(
                z_bf[:, cols(h), :].rearrange("p (c i) t -> p c t i", i=4),
                dif[:, :, cols(h)].rearrange("p t (c i) -> p c t i", i=4),
                gain[:].unsqueeze(1).unsqueeze(3).to_broadcast([P, HALF // 4, 4, 4]),
                ALU.mult)

        def z_quant(h):
            nc.vector.quantize_mx(z_w[:, cols(h)].bitcast(FP8X4), z_s[:, cols(h)], z_bf[:, cols(h), :].rearrange("p j t -> p (j t)"))

        def gate_half(e, h):
            gather(e, sg[:, 0, cols(h)], plane(6), half_list(l_n4, h))

        def gate_gather(e, t):
            gather(e, sg[:, t, :], plane(6 - t, 2), l_n4[:])

        def gate_product(t):
            nc.vector.scalar_tensor_tensor(prod[:, t, :], sg[:, t, :], 1.0, a_plane(t), ALU.subtract, ALU.mult)

        def join(t, cs):
            nc.vector.tensor_tensor(res[:, t, cs], g3[:, t, cs], prod[:, t, cs], ALU.add)

        def store(t):
            nc.sync.dma_start(out_rows[:, t, :], res[:, t, :])

        def fused_join(h):
            nc.vector.tensor_tensor(res[:, 3, cols(h)], a_last[:].indirect(half_list(l_n3, h)), prod[:, 3, cols(h)], ALU.add)

        def o_round(h):
            copy = nc.scalar.copy if h == 0 else nc.vector.tensor_copy
            copy(
                o_bf[h][:].rearrange("p (c i) t -> p c t i", i=4),
                res[:, :, cols(h)].rearrange("p t (c i) -> p c t i", i=4))

        def o_quant(h):
            nc.vector.quantize_mx(o_w[:, cols(h)].bitcast(FP8X4), o_s[:, cols(h)], o_bf[h][:].rearrange("p j t -> p (j t)"))
            nc.sync.dma_start(words_out[:, cols(h)], o_w[:, cols(h)].bitcast(I32))

        def y_out(t):
            nc.scalar.copy(y_sb[t][:], y_ps[t][:])

        whole = slice(0, S)
        y_out(0)
        y_out(1)
        y_gathers("S", 0, 0)
        y_gathers("S", 0, 1)
        y_out(3)
        y_gathers("S", 1, 0)
        y_out(2)
        y_gathers("S", 1, 1)
        y_gathers("S", 2, 0)
        y_gathers("S", 2, 1)
        z_top(0, whole)
        y_gathers("V", 3, 0)
        z_dif(0, whole)
        y_gathers("V", 3, 1)
        z_top(1, whole)
        z_top(3, whole)
        z_dif(1, whole)
        z_top(2, cols(0))
        z_dif(3, whole)
        z_dif(2, cols(0))
        z_top(2, cols(1))
        z_round(0)
        z_dif(2, cols(1))
        z_quant(0)
        z_round(1)
        for t in range(4):
            nc.scalar.activation(plane(6 - t), b_ps[t][:], ACT.Tanh, scale=-0.03125)
        gate_half("V", 1)
        z_quant(1)
        gate_gather("V", 3)
        gate_half("S", 0)
        for t in (1, 2):
            gate_gather("S", t)
        for t in (3, 0, 1, 2):
            a_ps = psum.tile([P, S], F32, name=f"a_ps{t}", tag=f"bank{4 + t}")
            nc.tensor.matmul_mx(
                a_ps[:], lhsT=w2w[:, 256 * t : 256 * (t + 1)].bitcast(FP4X4), lhsT_scale=w2s[:, P * t : P * (t + 1)],
                rhs=z_w[:].bitcast(FP8X4), rhs_scale=z_s[:], start=True, stop=True)
            nc.scalar.activation(a_plane(t), a_ps[:], ACT.Copy, scale=-0.5)
        for t in range(2):
            gather("S", g3[:, t, :], plane(2 - t, 2), l_n3[:])
        for h in range(2):
            gather("S", g3[:, 2, cols(h)], plane(0), half_list(l_n3, h))
        gate_product(3)
        gate_product(0)
        fused_join(0)
        gate_product(1)
        fused_join(1)
        store(3)
        gate_product(2)
        join(0, whole)
        store(0)
        join(1, whole)
        store(1)
        join(2, cols(0))
        o_round(0)
        join(2, cols(1))
        store(2)
        o_round(1)
        o_quant(0)
        o_quant(1)
        for q in range(4):
            queue = nc.sync if q % 2 == 0 else nc.scalar
            queue.dma_start(out_2[0, 4 * q : 4 * q + 4, :].bitcast(I32), o_s[32 * q : 32 * q + 4, :].bitcast(I32))
